import numpy as np
import ml_dtypes


def mxq(x, axis, fmt="e4m3"):
    dtype, down = {"e4m3": (ml_dtypes.float8_e4m3fn, 7), "e5m2": (ml_dtypes.float8_e5m2, 14)}[fmt]
    v = np.moveaxis(np.asarray(x, np.float32).astype(ml_dtypes.bfloat16).astype(np.float64), axis, -1)
    blocks = v.reshape(v.shape[:-1] + (-1, 32))
    amax = np.abs(blocks).max(-1, keepdims=True)
    byte = np.maximum(np.where(amax > 0, np.frexp(amax)[1] - 1 + 127, 0) - down, 1)
    scale = np.exp2(byte - 127.0)
    codes = (blocks / scale).astype(np.float32).astype(dtype).astype(np.float64)
    return np.moveaxis((codes * scale).reshape(v.shape), -1, axis)


WIDE = False


def mx_kscale(k):
    if not WIDE:
        return np.ones(k)
    levels = np.array([10, -10, 5, -5, 0])
    if k % 512:
        return np.exp2(np.random.permutation(np.resize(levels, k // 32))).repeat(32)
    a = np.empty((k // 512, 16))
    for p in range(k // 512):
        a[p, :8] = np.random.permutation(np.resize(levels, 8))
        for g in range(8):
            far = levels[np.abs(levels - a[p, g]) >= 10]
            a[p, g + 8] = far[np.random.randint(len(far))]
    return np.exp2(a.ravel()).repeat(32)


def f64(x):
    return np.asarray(x).astype(np.float64)


E2M1 = np.array([0.0, 0.5, 1.0, 1.5, 2.0, 3.0, 4.0, 6.0, -0.0, -0.5, -1.0, -1.5, -2.0, -3.0, -4.0, -6.0])


def pack_weight(w, fmt):
    k, n = w.shape
    w = f64(np.asarray(w, np.float32).astype(ml_dtypes.bfloat16)).reshape(k // 32, 32, n)
    amax = np.abs(w).max(1)
    if fmt == "e4m3":
        byte = np.frexp(amax)[1] - 1 + 127 - 7
    else:
        mant, ex = np.frexp(amax / 6.0)
        byte = np.where(mant > 0.5, ex, ex - 1) + 127
    byte = np.clip(np.where(amax > 0, byte, 1), 1, 254)
    scaled = (w * np.exp2(127.0 - byte)[:, None, :]).reshape(k, n).astype(np.float32)
    by_word = np.ascontiguousarray(scaled.reshape(k // 512, 128, 4, n).transpose(0, 1, 3, 2))
    if fmt == "e4m3":
        words = by_word.astype(ml_dtypes.float8_e4m3fn).view(np.uint8)
    else:
        c = by_word.astype(ml_dtypes.float4_e2m1fn).view(np.uint8) & 0xF
        words = (c[..., 0::2] | (c[..., 1::2] << 4)).reshape(k // 512, 128, 2 * n)
    return np.ascontiguousarray(words), np.ascontiguousarray(byte.astype(np.uint8).reshape(k // 512, 16, n))


def unpack_weight(words, scales, fmt):
    g, _, n = scales.shape
    words = np.ascontiguousarray(words).reshape(g, 128, n, -1)
    if fmt == "e4m3":
        vals = words.view(ml_dtypes.float8_e4m3fn).astype(np.float64)
    else:
        nib = np.empty((g, 128, n, 4), np.uint8)
        nib[..., 0::2] = words & 0xF
        nib[..., 1::2] = words >> 4
        vals = E2M1[nib]
    vals = vals * np.repeat(np.exp2(scales.astype(np.float64) - 127.0), 8, axis=1)[..., None]
    return vals.transpose(0, 1, 3, 2).reshape(g * 512, n)


def sigmoid(v):
    return 1.0 / (1.0 + np.exp(-v))


def bf(x):
    return np.asarray(x, np.float32).astype(ml_dtypes.bfloat16)


def planes(Y):
    r, m = Y.shape
    b = f64(bf(Y)).reshape(r // 32, 32, m)
    amax = np.abs(b).max(1)
    byte = np.clip(np.where(amax > 0, np.frexp(amax)[1] - 1 + 127 - 7, 1), 1, 254)
    codes = (b * np.exp2(127.0 - byte)[:, None, :]).reshape(r, m).astype(np.float32).astype(ml_dtypes.float8_e4m3fn).view(np.uint8)
    words = codes.reshape(r // 512, 128, 4, m).transpose(0, 1, 3, 2)
    return np.ascontiguousarray(words), np.ascontiguousarray(byte.astype(np.uint8).reshape(r // 512, 16, m))


K, L, M, T, N = 1024, 1024, 512, 512, 512


def setup_inputs():
    n = np.random.standard_normal
    fk = mx_kscale(K)
    fl = mx_kscale(L)
    fm = mx_kscale(M)
    wap = pack_weight(n((K, N)) * 1 / np.sqrt(K) * fk[:, None], "e2m1")
    xqp = pack_weight(n((L, T)) / fl[:, None], "e4m3")
    wqp = pack_weight(n((L, N)) * 1 / np.sqrt(L) * fl[:, None], "e2m1")
    xgp = pack_weight(n((M, T)) / fm[:, None], "e2m1")
    wgp = pack_weight(n((M, N)) * 1 / np.sqrt(M) * fm[:, None], "e4m3")
    return {
        "xa": (n((K, T)) / fk[:, None]).astype(np.float32),
        "wa_words": wap[0],
        "wa_scales": wap[1],
        "xq_words": xqp[0],
        "xq_scales": xqp[1],
        "wq_words": wqp[0],
        "wq_scales": wqp[1],
        "xg_words": xgp[0],
        "xg_scales": xgp[1],
        "wg_words": wgp[0],
        "wg_scales": wgp[1],
    }


def reference(xa, wa_words, wa_scales, xq_words, xq_scales, wq_words, wq_scales, xg_words, xg_scales, wg_words, wg_scales):
    wau = unpack_weight(wa_words, wa_scales, "e2m1")
    xqu = unpack_weight(xq_words, xq_scales, "e4m3")
    wqu = unpack_weight(wq_words, wq_scales, "e2m1")
    xgu = unpack_weight(xg_words, xg_scales, "e2m1")
    wgu = unpack_weight(wg_words, wg_scales, "e4m3")
    xaq = mxq(f64(xa), 0, "e4m3")
    p = wau.T @ xaq + wqu.T @ xqu
    g = wgu.T @ xgu
    y = p * sigmoid(g) + 0.1 * g
    words, scales = planes(y)
    return y, words, scales

@@ -1,0 +1,246 @@
+from contextlib import ExitStack
+
+import concourse.mybir as mybir
+from concourse.masks import make_identity
+
+K, L, M, T, N = 1024, 1024, 512, 512, 512
+FLOPS = 2 * (K + L + M) * T * N
+
+F32 = mybir.dt.float32
+BF16 = mybir.dt.bfloat16
+I32 = mybir.dt.int32
+U32 = mybir.dt.uint32
+U8 = mybir.dt.uint8
+FP8X4 = mybir.dt.float8_e4m3fn_x4
+FP4X4 = mybir.dt.float4_e2m1fn_x4
+ACT = mybir.ActivationFunctionType
+ALU = mybir.AluOpType
+
+P = 128
+PACK = 4
+TT = 128
+HALF = 256
+WG_COL, XG_COL, WA_COL, WQ_COL, XQ_COL = 0, 512, 1024, 2048, 3072
+PLANE_COLS = 4096
+
+
+def tile_mix_gate_over_mixed_sum_pl_kernel(
+    tc, xa, wa_words, wa_scales, xq_words, xq_scales, wq_words, wq_scales, xg_words, xg_scales, wg_words, wg_scales, out_0, out_1, out_2
+):
+    nc = tc.nc
+    with ExitStack() as ctx:
+        sb = ctx.enter_context(tc.tile_pool(name="sb", bufs=1))
+        ps = ctx.enter_context(tc.psum_pool(name="ps", bufs=1))
+        ctx.enter_context(tc.manual_schedule())
+
+        stage = sb.tile([16, PLANE_COLS], U8, name="stage")
+        planes = sb.tile([P, PLANE_COLS], U8, name="planes", align_bytes=64)
+        xg_sb = sb.tile([P, 2 * T], U8, name="xg_sb", align_bytes=64)
+        wg_sb = sb.tile([P, N], U32, name="wg_sb", align_bytes=64)
+        wa_sb = sb.tile([P, 2, 2 * N], U8, name="wa_sb", align_bytes=64)
+        wq_sb = sb.tile([P, 2, 2 * N], U8, name="wq_sb", align_bytes=64)
+        xq_sb = [sb.tile([P, 2, HALF], U32, name="xq_sb%d" % h, align_bytes=64) for h in range(2)]
+        raw = {(z, h): sb.tile([P, PACK, HALF], F32, name="raw%d%d" % (z, h)) for z in range(2) for h in range(2)}
+        xa_bf = {(z, j): sb.tile([P, TT * PACK], BF16, name="xa_bf%d%d" % (z, j), align_bytes=64) for z in range(2) for j in range(4)}
+        xa_codes = {(z, j): sb.tile([P, TT], U32, name="xa_codes%d%d" % (z, j), align_bytes=64) for z in range(2) for j in range(4)}
+        xa_scale = {(z, j): sb.tile([P, TT], U8, name="xa_scale%d%d" % (z, j), align_bytes=64) for z in range(2) for j in range(4)}
+        sig = [sb.tile([P, PACK, P], F32, name="sig%d" % j) for j in range(4)]
+        tenth = {j: sb.tile([P, PACK, P], F32, name="tenth%d" % j) for j in (2, 3)}
+        prod = [sb.tile([P, PACK, P], F32, name="prod%d" % j) for j in range(4)]
+        yt = {j: sb.tile([P, PACK, P], F32, name="yt%d" % j) for j in (0, 1)}
+        y_sb = [sb.tile([P, PACK, TT], F32, name="y_sb%d" % j) for j in range(4)]
+        y_bf = [sb.tile([P, TT * PACK], BF16, name="y_bf%d" % j, align_bytes=64) for j in range(4)]
+        y_codes = sb.tile([P, T], U32, name="y_codes", align_bytes=64)
+        y_scale = sb.tile([P, T], U8, name="y_scale", align_bytes=64)
+        ident = sb.tile([P, P], F32, name="ident")
+        warm = sb.tile([P, 2], F32, name="warm")
+        g_ps, p_ps, y_ps = {}, {}, {}
+
+        def load_stage(scales, col):
+            width = scales.shape[0] * 512
+            dst = stage[:, col : col + width].bitcast(I32).rearrange("q (z c) -> q z c", c=128)
+            nc.sync.dma_start(out=dst, in_=scales.bitcast(I32).rearrange("z q c -> q z c"))
+
+        def load_xa(z, h):
+            rows = xa[512 * z : 512 * (z + 1), HALF * h : HALF * (h + 1)]
+            nc.sync.dma_start(out=raw[z, h][:], in_=rows.rearrange("(p i) t -> p i t", i=PACK))
+
+        def load_xq(h):
+            src = xq_words.rearrange("z p t r -> p z (t r)")[:, :, 4 * HALF * h : 4 * HALF * (h + 1)]
+            nc.sync.dma_start(out=xq_sb[h][:].bitcast(I32), in_=src.bitcast(I32))
+
+        def interleave(copy, dst, src):
+            copy(out=dst.rearrange("p (c i r) -> p c r i", i=4, r=PACK), in_=src.rearrange("p r (c i) -> p c r i", i=4))
+
+        def cast_xa(copy, z, j):
+            t0 = TT * (j % 2)
+            interleave(copy, xa_bf[z, j][:], raw[z, j // 2][:, :, t0 : t0 + TT])
+
+        def quant_xa(z, j):
+            nc.vector.quantize_mx(out=xa_codes[z, j][:].bitcast(FP8X4), scales=xa_scale[z, j][:], in_=xa_bf[z, j][:])
+
+        def mm_g(j):
+            g_ps[j] = ps.tile([P, N], F32, name="g_ps%d" % j, tag="gy%d" % j)
+            nc.tensor.matmul_mx(
+                out=g_ps[j][:],
+                lhsT=xg_sb[:, 2 * TT * j : 2 * TT * (j + 1)].bitcast(FP4X4),
+                lhsT_scale=planes[:, XG_COL + TT * j : XG_COL + TT * (j + 1)],
+                rhs=wg_sb[:].bitcast(FP8X4),
+                rhs_scale=planes[:, WG_COL : WG_COL + N],
+                start=True,
+                stop=True,
+            )
+
+        def mm_a(z, j):
+            if z == 0:
+                p_ps[j] = ps.tile([P, N], F32, name="p_ps%d" % j, tag="p%d" % j)
+            nc.tensor.matmul_mx(
+                out=p_ps[j][:],
+                lhsT=xa_codes[z, j][:].bitcast(FP8X4),
+                lhsT_scale=xa_scale[z, j][:],
+                rhs=wa_sb[:, z, :].bitcast(FP4X4),
+                rhs_scale=planes[:, WA_COL + N * z : WA_COL + N * (z + 1)],
+                start=(z == 0),
+                stop=False,
+            )
+
+        def mm_q(j):
+            t0 = TT * (j % 2)
+            for z in range(2):
+                col = XQ_COL + T * z + TT * j
+                nc.tensor.matmul_mx(
+                    out=p_ps[j][:],
+                    lhsT=xq_sb[j // 2][:, z, t0 : t0 + TT].bitcast(FP8X4),
+                    lhsT_scale=planes[:, col : col + TT],
+                    rhs=wq_sb[:, z, :].bitcast(FP4X4),
+                    rhs_scale=planes[:, WQ_COL + N * z : WQ_COL + N * (z + 1)],
+                    start=False,
+                    stop=(z == 1),
+                )
+
+        def dealt(bank):
+            return bank[:].rearrange("t (m r) -> t r m", r=PACK)
+
+        def sigmoid(j):
+            nc.scalar.activation(out=sig[j][:], in_=dealt(g_ps[j]), func=ACT.Sigmoid)
+
+        def tenth_g(j):
+            nc.scalar.activation(out=tenth[j][:], in_=dealt(g_ps[j]), func=ACT.Copy, scale=0.1)
+
+        def gate(j):
+            nc.vector.tensor_tensor(out=prod[j][:], in0=dealt(p_ps[j]), in1=sig[j][:], op=ALU.mult)
+
+        def add_tenth(j):
+            nc.vector.scalar_tensor_tensor(out=yt[j][:], in0=dealt(g_ps[j]), scalar=0.1, in1=prod[j][:], op0=ALU.mult, op1=ALU.add)
+
+        def turn(j, src, first, last):
+            if first:
+                y_ps[j] = ps.tile([P, PACK, TT], F32, name="y_ps%d" % j, tag="gy%d" % j)
+            for r in range(PACK):
+                nc.tensor.matmul(
+                    out=y_ps[j][:, r, :], lhsT=src[:, r, :], rhs=ident[:], is_transpose=True, start=(first and r == 0), stop=(last and r == PACK - 1)
+                )
+
+        def copy_out(j):
+            nc.scalar.copy(out=y_sb[j][:], in_=y_ps[j][:])
+            dst = out_0[:, TT * j : TT * (j + 1)].rearrange("(p r) t -> p r t", r=PACK)
+            nc.sync.dma_start(out=dst, in_=y_sb[j][:])
+
+        def round_y(copy, j):
+            interleave(copy, y_bf[j][:], y_sb[j][:])
+
+        def quant_y(j):
+            cols = slice(TT * j, TT * (j + 1))
+            nc.vector.quantize_mx(out=y_codes[:, cols].bitcast(FP8X4), scales=y_scale[:, cols], in_=y_bf[j][:])
+
+        def store_words(j0, j1):
+            dst = out_1.rearrange("z p t r -> p (z t r)").bitcast(I32)
+            nc.sync.dma_start(out=dst[:, TT * j0 : TT * j1], in_=y_codes[:, TT * j0 : TT * j1].bitcast(I32))
+
+        v_copy, s_copy = nc.vector.tensor_copy, nc.scalar.copy
+
+        nc.vector.memset(planes[:].bitcast(I32), 0)
+        nc.gpsimd.memset(warm[:], 0.0)
+        make_identity(nc, ident[:])
+        nc.scalar.activation(out=warm[:, 1:2], in_=warm[:, 0:1], func=ACT.Sigmoid)
+
+        load_stage(wg_scales, WG_COL)
+        load_stage(xg_scales, XG_COL)
+        load_stage(wa_scales, WA_COL)
+        load_stage(wq_scales, WQ_COL)
+        load_stage(xq_scales, XQ_COL)
+        nc.sync.dma_start(out=xg_sb[:].bitcast(I32), in_=xg_words[0].bitcast(I32))
+        nc.sync.dma_start(out=wg_sb[:].bitcast(I32), in_=wg_words[0].rearrange("p n r -> p (n r)").bitcast(I32))
+        load_xa(0, 0)
+        for q in range(4):
+            nc.sync.dma_start(out=planes[32 * q : 32 * q + 4, :].bitcast(I32), in_=stage[4 * q : 4 * q + 4, :].bitcast(I32))
+        load_xa(1, 0)
+        nc.sync.dma_start(out=wa_sb[:].bitcast(I32), in_=wa_words.rearrange("z p c -> p z c").bitcast(I32))
+        nc.sync.dma_start(out=wq_sb[:].bitcast(I32), in_=wq_words.rearrange("z p c -> p z c").bitcast(I32))
+        load_xq(0)
+        load_xa(0, 1)
+        load_xa(1, 1)
+        load_xq(1)
+
+        cast_xa(v_copy, 0, 0)
+        cast_xa(s_copy, 0, 1)
+        quant_xa(0, 0)
+        quant_xa(0, 1)
+        for j in range(4):
+            mm_g(j)
+        cast_xa(v_copy, 1, 0)
+        cast_xa(v_copy, 1, 1)
+        quant_xa(1, 0)
+        quant_xa(1, 1)
+        sigmoid(0)
+        sigmoid(1)
+        for j in (2, 3):
+            sigmoid(j)
+            tenth_g(j)
+        for j in (0, 1):
+            mm_a(0, j)
+            mm_a(1, j)
+            mm_q(j)
+        gate(0)
+        cast_xa(v_copy, 0, 2)
+        add_tenth(0)
+        quant_xa(0, 2)
+        cast_xa(s_copy, 0, 3)
+        turn(0, yt[0], True, True)
+        turn(2, tenth[2], True, False)
+        gate(1)
+        quant_xa(0, 3)
+        add_tenth(1)
+        copy_out(0)
+        mm_a(0, 2)
+        mm_a(0, 3)
+        turn(1, yt[1], True, True)
+        turn(3, tenth[3], True, False)
+        cast_xa(v_copy, 1, 2)
+        cast_xa(s_copy, 1, 3)
+        round_y(v_copy, 0)
+        quant_xa(1, 2)
+        quant_xa(1, 3)
+        copy_out(1)
+        mm_a(1, 2)
+        mm_q(2)
+        mm_a(1, 3)
+        mm_q(3)
+        quant_y(0)
+        round_y(s_copy, 1)
+        gate(2)
+        quant_y(1)
+        store_words(0, 2)
+        gate(3)
+        turn(2, prod[2], False, True)
+        copy_out(2)
+        turn(3, prod[3], False, True)
+        round_y(v_copy, 2)
+        copy_out(3)
+        quant_y(2)
+        round_y(v_copy, 3)
+        quant_y(3)
+        store_words(2, 4)
+        for q in range(4):
+            queue = nc.scalar if q % 2 else nc.sync
+            queue.dma_start(out=out_2[0, 4 * q : 4 * q + 4, :].bitcast(I32), in_=y_scale[32 * q : 32 * q + 4, :].bitcast(I32))

@@ -33,22 +33,26 @@ def tile_mix_gate_over_mixed_sum_pl_kernel(
         ps = ctx.enter_context(tc.psum_pool(name="ps", bufs=1))
         ctx.enter_context(tc.manual_schedule())
 
-        stage = sb.tile([16, PLANE_COLS], U8, name="stage")
+        stage = sb.tile([32, PLANE_COLS], U8, name="stage")
         planes = sb.tile([P, PLANE_COLS], U8, name="planes", align_bytes=64)
         xg_sb = sb.tile([P, 2 * T], U8, name="xg_sb", align_bytes=64)
         wg_sb = sb.tile([P, N], U32, name="wg_sb", align_bytes=64)
         wa_sb = sb.tile([P, 2, 2 * N], U8, name="wa_sb", align_bytes=64)
         wq_sb = sb.tile([P, 2, 2 * N], U8, name="wq_sb", align_bytes=64)
         xq_sb = [sb.tile([P, 2, HALF], U32, name="xq_sb%d" % h, align_bytes=64) for h in range(2)]
-        raw = {(z, h): sb.tile([P, PACK, HALF], F32, name="raw%d%d" % (z, h)) for z in range(2) for h in range(2)}
+        pieces = [(0, 0, 2), (1, 0, 2), (0, 2, 4), (1, 2, 3), (1, 3, 4)]
+        raw_tile = {(z, j0): sb.tile([P, PACK, TT * (j1 - j0)], F32, name="raw%d%d" % (z, j0)) for z, j0, j1 in pieces}
+        raw = {(z, j): raw_tile[z, j0][:, :, TT * (j - j0) : TT * (j - j0 + 1)] for z, j0, j1 in pieces for j in range(j0, j1)}
         xa_bf = {(z, j): sb.tile([P, TT * PACK], BF16, name="xa_bf%d%d" % (z, j), align_bytes=64) for z in range(2) for j in range(4)}
         xa_codes = {(z, j): sb.tile([P, TT], U32, name="xa_codes%d%d" % (z, j), align_bytes=64) for z in range(2) for j in range(4)}
         xa_scale = {(z, j): sb.tile([P, TT], U8, name="xa_scale%d%d" % (z, j), align_bytes=64) for z in range(2) for j in range(4)}
         sig = [sb.tile([P, PACK, P], F32, name="sig%d" % j) for j in range(4)]
         tenth = {j: sb.tile([P, PACK, P], F32, name="tenth%d" % j) for j in (2, 3)}
-        prod = [sb.tile([P, PACK, P], F32, name="prod%d" % j) for j in range(4)]
         yt = {j: sb.tile([P, PACK, P], F32, name="yt%d" % j) for j in (0, 1)}
-        y_sb = [sb.tile([P, PACK, TT], F32, name="y_sb%d" % j) for j in range(4)]
+        prod = [sb.tile([P, PACK, P], F32, name="prod%d" % j) for j in range(4)]
+        y_pair = sb.tile([P, PACK, 2 * TT], F32, name="y_pair")
+        y_last = [sb.tile([P, PACK, TT], F32, name="y_last%d" % j) for j in range(2)]
+        y_sb = [y_pair[:, :, 0:TT], y_pair[:, :, TT : 2 * TT], y_last[0][:], y_last[1][:]]
         y_bf = [sb.tile([P, TT * PACK], BF16, name="y_bf%d" % j, align_bytes=64) for j in range(4)]
         y_codes = sb.tile([P, T], U32, name="y_codes", align_bytes=64)
         y_scale = sb.tile([P, T], U8, name="y_scale", align_bytes=64)
@@ -56,14 +60,14 @@ def tile_mix_gate_over_mixed_sum_pl_kernel(
         warm = sb.tile([P, 2], F32, name="warm")
         g_ps, p_ps, y_ps = {}, {}, {}
 
-        def load_stage(scales, col):
+        def load_stage(queue, scales, col):
             width = scales.shape[0] * 512
-            dst = stage[:, col : col + width].bitcast(I32).rearrange("q (z c) -> q z c", c=128)
-            nc.sync.dma_start(out=dst, in_=scales.bitcast(I32).rearrange("z q c -> q z c"))
+            dst = stage[16:32, col : col + width].bitcast(I32).rearrange("q (z c) -> q z c", c=128)
+            queue.dma_start(out=dst, in_=scales.bitcast(I32).rearrange("z q c -> q z c"))
 
-        def load_xa(z, h):
-            rows = xa[512 * z : 512 * (z + 1), HALF * h : HALF * (h + 1)]
-            nc.sync.dma_start(out=raw[z, h][:], in_=rows.rearrange("(p i) t -> p i t", i=PACK))
+        def load_xa(z, j0, j1):
+            rows = xa[512 * z : 512 * (z + 1), TT * j0 : TT * j1]
+            nc.sync.dma_start(out=raw_tile[z, j0][:], in_=rows.rearrange("(p i) t -> p i t", i=PACK))
 
         def load_xq(h):
             src = xq_words.rearrange("z p t r -> p z (t r)")[:, :, 4 * HALF * h : 4 * HALF * (h + 1)]
@@ -73,8 +77,7 @@ def tile_mix_gate_over_mixed_sum_pl_kernel(
             copy(out=dst.rearrange("p (c i r) -> p c r i", i=4, r=PACK), in_=src.rearrange("p r (c i) -> p c r i", i=4))
 
         def cast_xa(copy, z, j):
-            t0 = TT * (j % 2)
-            interleave(copy, xa_bf[z, j][:], raw[z, j // 2][:, :, t0 : t0 + TT])
+            interleave(copy, xa_bf[z, j][:], raw[z, j])
 
         def quant_xa(z, j):
             nc.vector.quantize_mx(out=xa_codes[z, j][:].bitcast(FP8X4), scales=xa_scale[z, j][:], in_=xa_bf[z, j][:])
@@ -91,8 +94,8 @@ def tile_mix_gate_over_mixed_sum_pl_kernel(
                 stop=True,
             )
 
-        def mm_a(z, j):
-            if z == 0:
+        def mm_a(z, j, first, last):
+            if first:
                 p_ps[j] = ps.tile([P, N], F32, name="p_ps%d" % j, tag="p%d" % j)
             nc.tensor.matmul_mx(
                 out=p_ps[j][:],
@@ -100,11 +103,13 @@ def tile_mix_gate_over_mixed_sum_pl_kernel(
                 lhsT_scale=xa_scale[z, j][:],
                 rhs=wa_sb[:, z, :].bitcast(FP4X4),
                 rhs_scale=planes[:, WA_COL + N * z : WA_COL + N * (z + 1)],
-                start=(z == 0),
-                stop=False,
+                start=first,
+                stop=last,
             )
 
-        def mm_q(j):
+        def mm_q(j, first, last):
+            if first:
+                p_ps[j] = ps.tile([P, N], F32, name="p_ps%d" % j, tag="p%d" % j)
             t0 = TT * (j % 2)
             for z in range(2):
                 col = XQ_COL + T * z + TT * j
@@ -114,8 +119,8 @@ def tile_mix_gate_over_mixed_sum_pl_kernel(
                     lhsT_scale=planes[:, col : col + TT],
                     rhs=wq_sb[:, z, :].bitcast(FP4X4),
                     rhs_scale=planes[:, WQ_COL + N * z : WQ_COL + N * (z + 1)],
-                    start=False,
-                    stop=(z == 1),
+                    start=(first and z == 0),
+                    stop=(last and z == 1),
                 )
 
         def dealt(bank):
@@ -125,13 +130,13 @@ def tile_mix_gate_over_mixed_sum_pl_kernel(
             nc.scalar.activation(out=sig[j][:], in_=dealt(g_ps[j]), func=ACT.Sigmoid)
 
         def tenth_g(j):
-            nc.scalar.activation(out=tenth[j][:], in_=dealt(g_ps[j]), func=ACT.Copy, scale=0.1)
-
-        def gate(j):
-            nc.vector.tensor_tensor(out=prod[j][:], in0=dealt(p_ps[j]), in1=sig[j][:], op=ALU.mult)
+            nc.vector.tensor_scalar(out=tenth[j][:], in0=dealt(g_ps[j]), scalar1=0.1, scalar2=None, op0=ALU.mult)
 
         def add_tenth(j):
             nc.vector.scalar_tensor_tensor(out=yt[j][:], in0=dealt(g_ps[j]), scalar=0.1, in1=prod[j][:], op0=ALU.mult, op1=ALU.add)
+
+        def gate(j, r0=0, r1=PACK):
+            nc.vector.tensor_tensor(out=prod[j][:, r0:r1, :], in0=dealt(p_ps[j])[:, r0:r1, :], in1=sig[j][:, r0:r1, :], op=ALU.mult)
 
         def turn(j, src, first, last):
             if first:
@@ -142,12 +147,17 @@ def tile_mix_gate_over_mixed_sum_pl_kernel(
                 )
 
         def copy_out(j):
-            nc.scalar.copy(out=y_sb[j][:], in_=y_ps[j][:])
-            dst = out_0[:, TT * j : TT * (j + 1)].rearrange("(p r) t -> p r t", r=PACK)
-            nc.sync.dma_start(out=dst, in_=y_sb[j][:])
+            nc.scalar.copy(out=y_sb[j], in_=y_ps[j][:])
+
+        def store_y(j0, j1, src):
+            dst = out_0[:, TT * j0 : TT * j1].rearrange("(p r) t -> p r t", r=PACK)
+            nc.sync.dma_start(out=dst, in_=src[:])
 
         def round_y(copy, j):
-            interleave(copy, y_bf[j][:], y_sb[j][:])
+            interleave(copy, y_bf[j][:], y_sb[j])
+
+        def round_y_psum(j):
+            nc.scalar.copy(out=y_bf[j][:].rearrange("p (t r) -> p t r", r=PACK), in_=y_ps[j][:].rearrange("p r t -> p t r"))
 
         def quant_y(j):
             cols = slice(TT * j, TT * (j + 1))
@@ -162,25 +172,26 @@ def tile_mix_gate_over_mixed_sum_pl_kernel(
         nc.vector.memset(planes[:].bitcast(I32), 0)
         nc.gpsimd.memset(warm[:], 0.0)
         make_identity(nc, ident[:])
-        nc.scalar.activation(out=warm[:, 1:2], in_=warm[:, 0:1], func=ACT.Sigmoid)
 
-        load_stage(wg_scales, WG_COL)
-        load_stage(xg_scales, XG_COL)
-        load_stage(wa_scales, WA_COL)
-        load_stage(wq_scales, WQ_COL)
-        load_stage(xq_scales, XQ_COL)
+        load_stage(nc.sync, wg_scales, WG_COL)
+        load_stage(nc.scalar, wq_scales, WQ_COL)
+        load_stage(nc.sync, xg_scales, XG_COL)
+        load_stage(nc.scalar, xq_scales, XQ_COL)
+        load_stage(nc.sync, wa_scales, WA_COL)
+        nc.scalar.activation(out=warm[:, 1:2], in_=warm[:, 0:1], func=ACT.Sigmoid)
         nc.sync.dma_start(out=xg_sb[:].bitcast(I32), in_=xg_words[0].bitcast(I32))
         nc.sync.dma_start(out=wg_sb[:].bitcast(I32), in_=wg_words[0].rearrange("p n r -> p (n r)").bitcast(I32))
-        load_xa(0, 0)
+        load_xa(0, 0, 2)
         for q in range(4):
-            nc.sync.dma_start(out=planes[32 * q : 32 * q + 4, :].bitcast(I32), in_=stage[4 * q : 4 * q + 4, :].bitcast(I32))
-        load_xa(1, 0)
+            nc.sync.dma_start(out=planes[32 * q : 32 * q + 4, :].bitcast(I32), in_=stage[16 + 4 * q : 20 + 4 * q, :].bitcast(I32))
+        load_xa(1, 0, 2)
         nc.sync.dma_start(out=wa_sb[:].bitcast(I32), in_=wa_words.rearrange("z p c -> p z c").bitcast(I32))
         nc.sync.dma_start(out=wq_sb[:].bitcast(I32), in_=wq_words.rearrange("z p c -> p z c").bitcast(I32))
         load_xq(0)
-        load_xa(0, 1)
-        load_xa(1, 1)
+        load_xa(0, 2, 4)
         load_xq(1)
+        load_xa(1, 2, 3)
+        load_xa(1, 3, 4)
 
         cast_xa(v_copy, 0, 0)
         cast_xa(s_copy, 0, 1)
@@ -192,55 +203,58 @@ def tile_mix_gate_over_mixed_sum_pl_kernel(
         cast_xa(v_copy, 1, 1)
         quant_xa(1, 0)
         quant_xa(1, 1)
-        sigmoid(0)
-        sigmoid(1)
-        for j in (2, 3):
+        for j in range(4):
             sigmoid(j)
-            tenth_g(j)
         for j in (0, 1):
-            mm_a(0, j)
-            mm_a(1, j)
-            mm_q(j)
+            mm_a(0, j, True, False)
+            mm_a(1, j, False, False)
+            mm_q(j, False, True)
+        tenth_g(2)
         gate(0)
-        cast_xa(v_copy, 0, 2)
+        tenth_g(3)
         add_tenth(0)
-        quant_xa(0, 2)
+        cast_xa(s_copy, 0, 2)
         cast_xa(s_copy, 0, 3)
-        turn(0, yt[0], True, True)
         turn(2, tenth[2], True, False)
-        gate(1)
-        quant_xa(0, 3)
-        add_tenth(1)
-        copy_out(0)
-        mm_a(0, 2)
-        mm_a(0, 3)
-        turn(1, yt[1], True, True)
         turn(3, tenth[3], True, False)
+        turn(0, yt[0], True, True)
+        gate(1)
+        quant_xa(0, 2)
+        add_tenth(1)
+        quant_xa(0, 3)
+        copy_out(0)
+        mm_q(2, True, False)
+        mm_q(3, True, False)
+        turn(1, yt[1], True, True)
         cast_xa(v_copy, 1, 2)
         cast_xa(s_copy, 1, 3)
-        round_y(v_copy, 0)
+        round_y_psum(0)
         quant_xa(1, 2)
         quant_xa(1, 3)
+        mm_a(0, 2, False, False)
+        mm_a(1, 2, False, True)
+        mm_a(0, 3, False, False)
+        mm_a(1, 3, False, True)
         copy_out(1)
-        mm_a(1, 2)
-        mm_q(2)
-        mm_a(1, 3)
-        mm_q(3)
+        store_y(0, 2, y_pair)
         quant_y(0)
-        round_y(s_copy, 1)
+        round_y_psum(1)
         gate(2)
-        quant_y(1)
-        store_words(0, 2)
-        gate(3)
+        gate(3, 0, 2)
+        gate(3, 2, 4)
         turn(2, prod[2], False, True)
         copy_out(2)
+        store_y(2, 3, y_last[0])
         turn(3, prod[3], False, True)
+        quant_y(1)
+        store_words(0, 2)
         round_y(v_copy, 2)
         copy_out(3)
+        store_y(3, 4, y_last[1])
         quant_y(2)
         round_y(v_copy, 3)
         quant_y(3)
         store_words(2, 4)
         for q in range(4):
-            queue = nc.scalar if q % 2 else nc.sync
+            queue = nc.sync if q == 3 else nc.scalar
             queue.dma_start(out=out_2[0, 4 * q : 4 * q + 4, :].bitcast(I32), in_=y_scale[32 * q : 32 * q + 4, :].bitcast(I32))

@@ -39,26 +39,27 @@ def tile_mix_gate_over_mixed_sum_pl_kernel(
         wg_sb = sb.tile([P, N], U32, name="wg_sb", align_bytes=64)
         wa_sb = sb.tile([P, 2, 2 * N], U8, name="wa_sb", align_bytes=64)
         wq_sb = sb.tile([P, 2, 2 * N], U8, name="wq_sb", align_bytes=64)
-        xq_sb = [sb.tile([P, 2, HALF], U32, name="xq_sb%d" % h, align_bytes=64) for h in range(2)]
-        pieces = [(0, 0, 2), (1, 0, 2), (0, 2, 4), (1, 2, 3), (1, 3, 4)]
+        xq_pieces = [(0, 2), (2, 3), (3, 4)]
+        xq_tile = {j0: sb.tile([P, 2, TT * (j1 - j0)], U32, name="xq_sb%d" % j0, align_bytes=64) for j0, j1 in xq_pieces}
+        xq_sb = {j: xq_tile[j0][:, :, TT * (j - j0) : TT * (j - j0 + 1)] for j0, j1 in xq_pieces for j in range(j0, j1)}
+        pieces = [(0, 0, 1), (1, 0, 1), (0, 1, 2), (1, 1, 2), (0, 2, 4), (1, 2, 3), (1, 3, 4)]
         raw_tile = {(z, j0): sb.tile([P, PACK, TT * (j1 - j0)], F32, name="raw%d%d" % (z, j0)) for z, j0, j1 in pieces}
         raw = {(z, j): raw_tile[z, j0][:, :, TT * (j - j0) : TT * (j - j0 + 1)] for z, j0, j1 in pieces for j in range(j0, j1)}
         xa_bf = {(z, j): sb.tile([P, TT * PACK], BF16, name="xa_bf%d%d" % (z, j), align_bytes=64) for z in range(2) for j in range(4)}
         xa_codes = {(z, j): sb.tile([P, TT], U32, name="xa_codes%d%d" % (z, j), align_bytes=64) for z in range(2) for j in range(4)}
         xa_scale = {(z, j): sb.tile([P, TT], U8, name="xa_scale%d%d" % (z, j), align_bytes=64) for z in range(2) for j in range(4)}
         sig = [sb.tile([P, PACK, P], F32, name="sig%d" % j) for j in range(4)]
-        tenth = {j: sb.tile([P, PACK, P], F32, name="tenth%d" % j) for j in (2, 3)}
-        yt = {j: sb.tile([P, PACK, P], F32, name="yt%d" % j) for j in (0, 1)}
+        tenth = {j: sb.tile([P, PACK, P], F32, name="tenth%d" % j) for j in (1, 2, 3)}
+        yt = {0: sb.tile([P, PACK, P], F32, name="yt0")}
         prod = [sb.tile([P, PACK, P], F32, name="prod%d" % j) for j in range(4)]
-        y_pair = sb.tile([P, PACK, 2 * TT], F32, name="y_pair")
-        y_last = [sb.tile([P, PACK, TT], F32, name="y_last%d" % j) for j in range(2)]
-        y_sb = [y_pair[:, :, 0:TT], y_pair[:, :, TT : 2 * TT], y_last[0][:], y_last[1][:]]
+        y_tile = [sb.tile([P, PACK, TT], F32, name="y_sb%d" % j) for j in range(4)]
+        y_sb = [tile[:] for tile in y_tile]
         y_bf = [sb.tile([P, TT * PACK], BF16, name="y_bf%d" % j, align_bytes=64) for j in range(4)]
         y_codes = sb.tile([P, T], U32, name="y_codes", align_bytes=64)
         y_scale = sb.tile([P, T], U8, name="y_scale", align_bytes=64)
         ident = sb.tile([P, P], F32, name="ident")
         warm = sb.tile([P, 2], F32, name="warm")
-        g_ps, p_ps, y_ps = {}, {}, {}
+        g_ps, p_ps, y_ps, y_half = {}, {}, {}, []
 
         def load_stage(queue, scales, col):
             width = scales.shape[0] * 512
@@ -69,9 +70,9 @@ def tile_mix_gate_over_mixed_sum_pl_kernel(
             rows = xa[512 * z : 512 * (z + 1), TT * j0 : TT * j1]
             nc.sync.dma_start(out=raw_tile[z, j0][:], in_=rows.rearrange("(p i) t -> p i t", i=PACK))
 
-        def load_xq(h):
-            src = xq_words.rearrange("z p t r -> p z (t r)")[:, :, 4 * HALF * h : 4 * HALF * (h + 1)]
-            nc.sync.dma_start(out=xq_sb[h][:].bitcast(I32), in_=src.bitcast(I32))
+        def load_xq(j0, j1):
+            src = xq_words.rearrange("z p t r -> p z (t r)")[:, :, PACK * TT * j0 : PACK * TT * j1]
+            nc.sync.dma_start(out=xq_tile[j0][:].bitcast(I32), in_=src.bitcast(I32))
 
         def interleave(copy, dst, src):
             copy(out=dst.rearrange("p (c i r) -> p c r i", i=4, r=PACK), in_=src.rearrange("p r (c i) -> p c r i", i=4))
@@ -110,12 +111,11 @@ def tile_mix_gate_over_mixed_sum_pl_kernel(
         def mm_q(j, first, last):
             if first:
                 p_ps[j] = ps.tile([P, N], F32, name="p_ps%d" % j, tag="p%d" % j)
-            t0 = TT * (j % 2)
             for z in range(2):
                 col = XQ_COL + T * z + TT * j
                 nc.tensor.matmul_mx(
                     out=p_ps[j][:],
-                    lhsT=xq_sb[j // 2][:, z, t0 : t0 + TT].bitcast(FP8X4),
+                    lhsT=xq_sb[j][:, z, :].bitcast(FP8X4),
                     lhsT_scale=planes[:, col : col + TT],
                     rhs=wq_sb[:, z, :].bitcast(FP4X4),
                     rhs_scale=planes[:, WQ_COL + N * z : WQ_COL + N * (z + 1)],
@@ -139,6 +139,15 @@ def tile_mix_gate_over_mixed_sum_pl_kernel(
             nc.vector.tensor_tensor(out=prod[j][:, r0:r1, :], in0=dealt(p_ps[j])[:, r0:r1, :], in1=sig[j][:, r0:r1, :], op=ALU.mult)
 
         def turn(j, src, first, last):
+            if j == 3:
+                if first:
+                    y_half.append(ps.tile([P, 2, TT], F32, name="y_half0", tag="gy3"))
+                    y_half.append(ps.tile([P, 2, TT], F32, name="y_half1", tag="p0"))
+                for r in range(PACK):
+                    nc.tensor.matmul(
+                        out=y_half[r // 2][:, r % 2, :], lhsT=src[:, r, :], rhs=ident[:], is_transpose=True, start=(first and r % 2 == 0), stop=(last and r % 2 == 1)
+                    )
+                return
             if first:
                 y_ps[j] = ps.tile([P, PACK, TT], F32, name="y_ps%d" % j, tag="gy%d" % j)
             for r in range(PACK):
@@ -146,12 +155,16 @@ def tile_mix_gate_over_mixed_sum_pl_kernel(
                     out=y_ps[j][:, r, :], lhsT=src[:, r, :], rhs=ident[:], is_transpose=True, start=(first and r == 0), stop=(last and r == PACK - 1)
                 )
 
+        def copy_half(h):
+            copy = nc.vector.tensor_copy if h else nc.scalar.copy
+            copy(out=y_sb[3][:, 2 * h : 2 * h + 2, :], in_=y_half[h][:])
+
         def copy_out(j):
             nc.scalar.copy(out=y_sb[j], in_=y_ps[j][:])
 
         def store_y(j0, j1, src):
             dst = out_0[:, TT * j0 : TT * j1].rearrange("(p r) t -> p r t", r=PACK)
-            nc.sync.dma_start(out=dst, in_=src[:])
+            nc.sync.dma_start(out=dst, in_=src)
 
         def round_y(copy, j):
             interleave(copy, y_bf[j][:], y_sb[j])
@@ -181,80 +194,88 @@ def tile_mix_gate_over_mixed_sum_pl_kernel(
         nc.scalar.activation(out=warm[:, 1:2], in_=warm[:, 0:1], func=ACT.Sigmoid)
         nc.sync.dma_start(out=xg_sb[:].bitcast(I32), in_=xg_words[0].bitcast(I32))
         nc.sync.dma_start(out=wg_sb[:].bitcast(I32), in_=wg_words[0].rearrange("p n r -> p (n r)").bitcast(I32))
-        load_xa(0, 0, 2)
-        for q in range(4):
-            nc.sync.dma_start(out=planes[32 * q : 32 * q + 4, :].bitcast(I32), in_=stage[16 + 4 * q : 20 + 4 * q, :].bitcast(I32))
-        load_xa(1, 0, 2)
+        load_xa(0, 0, 1)
+        for r in range(4):
+            nc.sync.dma_start(out=planes[r:P:32, :].bitcast(I32), in_=stage[16 + r : 32 : 4, :].bitcast(I32))
+        load_xa(1, 0, 1)
         nc.sync.dma_start(out=wa_sb[:].bitcast(I32), in_=wa_words.rearrange("z p c -> p z c").bitcast(I32))
         nc.sync.dma_start(out=wq_sb[:].bitcast(I32), in_=wq_words.rearrange("z p c -> p z c").bitcast(I32))
-        load_xq(0)
+        load_xq(0, 2)
+        load_xa(0, 1, 2)
+        load_xa(1, 1, 2)
+        load_xq(2, 3)
         load_xa(0, 2, 4)
-        load_xq(1)
         load_xa(1, 2, 3)
         load_xa(1, 3, 4)
+        load_xq(3, 4)
 
         cast_xa(v_copy, 0, 0)
-        cast_xa(s_copy, 0, 1)
         quant_xa(0, 0)
-        quant_xa(0, 1)
         for j in range(4):
             mm_g(j)
         cast_xa(v_copy, 1, 0)
-        cast_xa(v_copy, 1, 1)
-        quant_xa(1, 0)
-        quant_xa(1, 1)
         for j in range(4):
             sigmoid(j)
-        for j in (0, 1):
-            mm_a(0, j, True, False)
-            mm_a(1, j, False, False)
-            mm_q(j, False, True)
+        quant_xa(1, 0)
+        mm_a(0, 0, True, False)
+        mm_a(1, 0, False, False)
+        mm_q(0, False, True)
+        mm_q(1, True, False)
+        tenth_g(1)
         tenth_g(2)
-        gate(0)
-        tenth_g(3)
-        add_tenth(0)
-        cast_xa(s_copy, 0, 2)
-        cast_xa(s_copy, 0, 3)
+        turn(1, tenth[1], True, False)
         turn(2, tenth[2], True, False)
+        gate(0)
+        cast_xa(s_copy, 0, 1)
+        tenth_g(3)
+        cast_xa(v_copy, 1, 1)
+        quant_xa(0, 1)
+        quant_xa(1, 1)
+        add_tenth(0)
+        mm_q(2, True, False)
+        mm_a(0, 1, False, False)
+        mm_a(1, 1, False, True)
         turn(3, tenth[3], True, False)
         turn(0, yt[0], True, True)
         gate(1)
-        quant_xa(0, 2)
-        add_tenth(1)
-        quant_xa(0, 3)
+        cast_xa(s_copy, 0, 2)
+        cast_xa(s_copy, 0, 3)
+        turn(1, prod[1], False, True)
         copy_out(0)
-        mm_q(2, True, False)
-        mm_q(3, True, False)
-        turn(1, yt[1], True, True)
+        store_y(0, 1, y_sb[0])
+        quant_xa(0, 2)
         cast_xa(v_copy, 1, 2)
-        cast_xa(s_copy, 1, 3)
-        round_y_psum(0)
+        quant_xa(0, 3)
         quant_xa(1, 2)
-        quant_xa(1, 3)
-        mm_a(0, 2, False, False)
-        mm_a(1, 2, False, True)
-        mm_a(0, 3, False, False)
-        mm_a(1, 3, False, True)
+        cast_xa(v_copy, 1, 3)
         copy_out(1)
-        store_y(0, 2, y_pair)
-        quant_y(0)
+        store_y(1, 2, y_sb[1])
+        round_y_psum(0)
+        mm_a(0, 2, False, False)
+        mm_a(0, 3, True, False)
+        mm_a(1, 2, False, True)
+        mm_q(3, False, False)
+        quant_xa(1, 3)
         round_y_psum(1)
         gate(2)
+        mm_a(1, 3, False, True)
+        turn(2, prod[2], False, True)
         gate(3, 0, 2)
         gate(3, 2, 4)
-        turn(2, prod[2], False, True)
-        copy_out(2)
-        store_y(2, 3, y_last[0])
-        turn(3, prod[3], False, True)
+        quant_y(0)
         quant_y(1)
         store_words(0, 2)
-        round_y(v_copy, 2)
-        copy_out(3)
-        store_y(3, 4, y_last[1])
-        quant_y(2)
+        copy_out(2)
+        store_y(2, 3, y_sb[2])
+        turn(3, prod[3], False, True)
+        copy_half(0)
+        copy_half(1)
+        store_y(3, 4, y_sb[3])
+        round_y_psum(2)
         round_y(v_copy, 3)
+        quant_y(2)
         quant_y(3)
         store_words(2, 4)
-        for q in range(4):
-            queue = nc.sync if q == 3 else nc.scalar
-            queue.dma_start(out=out_2[0, 4 * q : 4 * q + 4, :].bitcast(I32), in_=y_scale[32 * q : 32 * q + 4, :].bitcast(I32))
+        for r in range(4):
+            queue = nc.sync if r == 3 else nc.scalar
+            queue.dma_start(out=out_2[0, r:16:4, :].bitcast(I32), in_=y_scale[r:P:32, :].bitcast(I32))

from contextlib import ExitStack

import concourse.mybir as mybir
from concourse.masks import make_identity

K, L, M, T, N = 1024, 1024, 512, 512, 512
FLOPS = 2 * (K + L + M) * T * N

F32 = mybir.dt.float32
BF16 = mybir.dt.bfloat16
I32 = mybir.dt.int32
U32 = mybir.dt.uint32
U8 = mybir.dt.uint8
FP8X4 = mybir.dt.float8_e4m3fn_x4
FP4X4 = mybir.dt.float4_e2m1fn_x4
ACT = mybir.ActivationFunctionType
ALU = mybir.AluOpType

P = 128
PACK = 4
TT = 128
HALF = 256
WG_COL, XG_COL, WA_COL, WQ_COL, XQ_COL = 0, 512, 1024, 2048, 3072
PLANE_COLS = 4096


def tile_mix_gate_over_mixed_sum_pl_kernel(
    tc, xa, wa_words, wa_scales, xq_words, xq_scales, wq_words, wq_scales, xg_words, xg_scales, wg_words, wg_scales, out_0, out_1, out_2
):
    nc = tc.nc
    with ExitStack() as ctx:
        sb = ctx.enter_context(tc.tile_pool(name="sb", bufs=1))
        ps = ctx.enter_context(tc.psum_pool(name="ps", bufs=1))
        ctx.enter_context(tc.manual_schedule())

        stage = sb.tile([32, PLANE_COLS], U8, name="stage")
        planes = sb.tile([P, PLANE_COLS], U8, name="planes", align_bytes=64)
        xg_sb = sb.tile([P, 2 * T], U8, name="xg_sb", align_bytes=64)
        wg_sb = sb.tile([P, N], U32, name="wg_sb", align_bytes=64)
        wa_sb = sb.tile([P, 2, 2 * N], U8, name="wa_sb", align_bytes=64)
        wq_sb = sb.tile([P, 2, 2 * N], U8, name="wq_sb", align_bytes=64)
        xq_pieces = [(0, 2), (2, 3), (3, 4)]
        xq_tile = {j0: sb.tile([P, 2, TT * (j1 - j0)], U32, name="xq_sb%d" % j0, align_bytes=64) for j0, j1 in xq_pieces}
        xq_sb = {j: xq_tile[j0][:, :, TT * (j - j0) : TT * (j - j0 + 1)] for j0, j1 in xq_pieces for j in range(j0, j1)}
        pieces = [(0, 0, 1), (1, 0, 1), (0, 1, 2), (1, 1, 2), (0, 2, 4), (1, 2, 3), (1, 3, 4)]
        raw_tile = {(z, j0): sb.tile([P, PACK, TT * (j1 - j0)], F32, name="raw%d%d" % (z, j0)) for z, j0, j1 in pieces}
        raw = {(z, j): raw_tile[z, j0][:, :, TT * (j - j0) : TT * (j - j0 + 1)] for z, j0, j1 in pieces for j in range(j0, j1)}
        xa_bf = {(z, j): sb.tile([P, TT * PACK], BF16, name="xa_bf%d%d" % (z, j), align_bytes=64) for z in range(2) for j in range(4)}
        xa_codes = {(z, j): sb.tile([P, TT], U32, name="xa_codes%d%d" % (z, j), align_bytes=64) for z in range(2) for j in range(4)}
        xa_scale = {(z, j): sb.tile([P, TT], U8, name="xa_scale%d%d" % (z, j), align_bytes=64) for z in range(2) for j in range(4)}
        sig = [sb.tile([P, PACK, P], F32, name="sig%d" % j) for j in range(4)]
        tenth = {j: sb.tile([P, PACK, P], F32, name="tenth%d" % j) for j in (1, 2, 3)}
        yt = {0: sb.tile([P, PACK, P], F32, name="yt0")}
        prod = [sb.tile([P, PACK, P], F32, name="prod%d" % j) for j in range(4)]
        y_tile = [sb.tile([P, PACK, TT], F32, name="y_sb%d" % j) for j in range(4)]
        y_sb = [tile[:] for tile in y_tile]
        y_bf = [sb.tile([P, TT * PACK], BF16, name="y_bf%d" % j, align_bytes=64) for j in range(4)]
        y_codes = sb.tile([P, T], U32, name="y_codes", align_bytes=64)
        y_scale = sb.tile([P, T], U8, name="y_scale", align_bytes=64)
        ident = sb.tile([P, P], F32, name="ident")
        warm = sb.tile([P, 2], F32, name="warm")
        g_ps, p_ps, y_ps, y_half = {}, {}, {}, []

        def load_stage(queue, scales, col):
            width = scales.shape[0] * 512
            dst = stage[16:32, col : col + width].bitcast(I32).rearrange("q (z c) -> q z c", c=128)
            queue.dma_start(out=dst, in_=scales.bitcast(I32).rearrange("z q c -> q z c"))

        def load_xa(z, j0, j1):
            rows = xa[512 * z : 512 * (z + 1), TT * j0 : TT * j1]
            nc.sync.dma_start(out=raw_tile[z, j0][:], in_=rows.rearrange("(p i) t -> p i t", i=PACK))

        def load_xq(j0, j1):
            src = xq_words.rearrange("z p t r -> p z (t r)")[:, :, PACK * TT * j0 : PACK * TT * j1]
            nc.sync.dma_start(out=xq_tile[j0][:].bitcast(I32), in_=src.bitcast(I32))

        def interleave(copy, dst, src):
            copy(out=dst.rearrange("p (c i r) -> p c r i", i=4, r=PACK), in_=src.rearrange("p r (c i) -> p c r i", i=4))

        def cast_xa(copy, z, j):
            interleave(copy, xa_bf[z, j][:], raw[z, j])

        def quant_xa(z, j):
            nc.vector.quantize_mx(out=xa_codes[z, j][:].bitcast(FP8X4), scales=xa_scale[z, j][:], in_=xa_bf[z, j][:])

        def mm_g(j):
            g_ps[j] = ps.tile([P, N], F32, name="g_ps%d" % j, tag="gy%d" % j)
            nc.tensor.matmul_mx(
                out=g_ps[j][:],
                lhsT=xg_sb[:, 2 * TT * j : 2 * TT * (j + 1)].bitcast(FP4X4),
                lhsT_scale=planes[:, XG_COL + TT * j : XG_COL + TT * (j + 1)],
                rhs=wg_sb[:].bitcast(FP8X4),
                rhs_scale=planes[:, WG_COL : WG_COL + N],
                start=True,
                stop=True,
            )

        def mm_a(z, j, first, last):
            if first:
                p_ps[j] = ps.tile([P, N], F32, name="p_ps%d" % j, tag="p%d" % j)
            nc.tensor.matmul_mx(
                out=p_ps[j][:],
                lhsT=xa_codes[z, j][:].bitcast(FP8X4),
                lhsT_scale=xa_scale[z, j][:],
                rhs=wa_sb[:, z, :].bitcast(FP4X4),
                rhs_scale=planes[:, WA_COL + N * z : WA_COL + N * (z + 1)],
                start=first,
                stop=last,
            )

        def mm_q(j, first, last):
            if first:
                p_ps[j] = ps.tile([P, N], F32, name="p_ps%d" % j, tag="p%d" % j)
            for z in range(2):
                col = XQ_COL + T * z + TT * j
                nc.tensor.matmul_mx(
                    out=p_ps[j][:],
                    lhsT=xq_sb[j][:, z, :].bitcast(FP8X4),
                    lhsT_scale=planes[:, col : col + TT],
                    rhs=wq_sb[:, z, :].bitcast(FP4X4),
                    rhs_scale=planes[:, WQ_COL + N * z : WQ_COL + N * (z + 1)],
                    start=(first and z == 0),
                    stop=(last and z == 1),
                )

        def dealt(bank):
            return bank[:].rearrange("t (m r) -> t r m", r=PACK)

        def sigmoid(j):
            nc.scalar.activation(out=sig[j][:], in_=dealt(g_ps[j]), func=ACT.Sigmoid)

        def tenth_g(j):
            nc.vector.tensor_scalar(out=tenth[j][:], in0=dealt(g_ps[j]), scalar1=0.1, scalar2=None, op0=ALU.mult)

        def add_tenth(j):
            nc.vector.scalar_tensor_tensor(out=yt[j][:], in0=dealt(g_ps[j]), scalar=0.1, in1=prod[j][:], op0=ALU.mult, op1=ALU.add)

        def gate(j, r0=0, r1=PACK):
            nc.vector.tensor_tensor(out=prod[j][:, r0:r1, :], in0=dealt(p_ps[j])[:, r0:r1, :], in1=sig[j][:, r0:r1, :], op=ALU.mult)

        def turn(j, src, first, last):
            if j == 3:
                if first:
                    y_half.append(ps.tile([P, 2, TT], F32, name="y_half0", tag="gy3"))
                    y_half.append(ps.tile([P, 2, TT], F32, name="y_half1", tag="p0"))
                for r in range(PACK):
                    nc.tensor.matmul(
                        out=y_half[r // 2][:, r % 2, :], lhsT=src[:, r, :], rhs=ident[:], is_transpose=True, start=(first and r % 2 == 0), stop=(last and r % 2 == 1)
                    )
                return
            if first:
                y_ps[j] = ps.tile([P, PACK, TT], F32, name="y_ps%d" % j, tag="gy%d" % j)
            for r in range(PACK):
                nc.tensor.matmul(
                    out=y_ps[j][:, r, :], lhsT=src[:, r, :], rhs=ident[:], is_transpose=True, start=(first and r == 0), stop=(last and r == PACK - 1)
                )

        def copy_half(h):
            copy = nc.vector.tensor_copy if h else nc.scalar.copy
            copy(out=y_sb[3][:, 2 * h : 2 * h + 2, :], in_=y_half[h][:])

        def copy_out(j):
            nc.scalar.copy(out=y_sb[j], in_=y_ps[j][:])

        def store_y(j0, j1, src):
            dst = out_0[:, TT * j0 : TT * j1].rearrange("(p r) t -> p r t", r=PACK)
            nc.sync.dma_start(out=dst, in_=src)

        def round_y(copy, j):
            interleave(copy, y_bf[j][:], y_sb[j])

        def round_y_psum(j):
            nc.scalar.copy(out=y_bf[j][:].rearrange("p (t r) -> p t r", r=PACK), in_=y_ps[j][:].rearrange("p r t -> p t r"))

        def quant_y(j):
            cols = slice(TT * j, TT * (j + 1))
            nc.vector.quantize_mx(out=y_codes[:, cols].bitcast(FP8X4), scales=y_scale[:, cols], in_=y_bf[j][:])

        def store_words(j0, j1):
            dst = out_1.rearrange("z p t r -> p (z t r)").bitcast(I32)
            nc.sync.dma_start(out=dst[:, TT * j0 : TT * j1], in_=y_codes[:, TT * j0 : TT * j1].bitcast(I32))

        v_copy, s_copy = nc.vector.tensor_copy, nc.scalar.copy

        nc.vector.memset(planes[:].bitcast(I32), 0)
        nc.gpsimd.memset(warm[:], 0.0)
        make_identity(nc, ident[:])

        load_stage(nc.sync, wg_scales, WG_COL)
        load_stage(nc.scalar, wq_scales, WQ_COL)
        load_stage(nc.sync, xg_scales, XG_COL)
        load_stage(nc.scalar, xq_scales, XQ_COL)
        load_stage(nc.sync, wa_scales, WA_COL)
        nc.scalar.activation(out=warm[:, 1:2], in_=warm[:, 0:1], func=ACT.Sigmoid)
        nc.sync.dma_start(out=xg_sb[:].bitcast(I32), in_=xg_words[0].bitcast(I32))
        nc.sync.dma_start(out=wg_sb[:].bitcast(I32), in_=wg_words[0].rearrange("p n r -> p (n r)").bitcast(I32))
        load_xa(0, 0, 1)
        for r in range(4):
            nc.sync.dma_start(out=planes[r:P:32, :].bitcast(I32), in_=stage[16 + r : 32 : 4, :].bitcast(I32))
        load_xa(1, 0, 1)
        nc.sync.dma_start(out=wa_sb[:].bitcast(I32), in_=wa_words.rearrange("z p c -> p z c").bitcast(I32))
        nc.sync.dma_start(out=wq_sb[:].bitcast(I32), in_=wq_words.rearrange("z p c -> p z c").bitcast(I32))
        load_xq(0, 2)
        load_xa(0, 1, 2)
        load_xa(1, 1, 2)
        load_xq(2, 3)
        load_xa(0, 2, 4)
        load_xa(1, 2, 3)
        load_xa(1, 3, 4)
        load_xq(3, 4)

        cast_xa(v_copy, 0, 0)
        quant_xa(0, 0)
        for j in range(4):
            mm_g(j)
        cast_xa(v_copy, 1, 0)
        for j in range(4):
            sigmoid(j)
        quant_xa(1, 0)
        mm_a(0, 0, True, False)
        mm_a(1, 0, False, False)
        mm_q(0, False, True)
        mm_q(1, True, False)
        tenth_g(1)
        tenth_g(2)
        turn(1, tenth[1], True, False)
        turn(2, tenth[2], True, False)
        gate(0)
        cast_xa(s_copy, 0, 1)
        tenth_g(3)
        cast_xa(v_copy, 1, 1)
        quant_xa(0, 1)
        quant_xa(1, 1)
        add_tenth(0)
        mm_q(2, True, False)
        mm_a(0, 1, False, False)
        mm_a(1, 1, False, True)
        turn(3, tenth[3], True, False)
        turn(0, yt[0], True, True)
        gate(1)
        cast_xa(s_copy, 0, 2)
        cast_xa(s_copy, 0, 3)
        turn(1, prod[1], False, True)
        copy_out(0)
        store_y(0, 1, y_sb[0])
        quant_xa(0, 2)
        cast_xa(v_copy, 1, 2)
        quant_xa(0, 3)
        quant_xa(1, 2)
        cast_xa(v_copy, 1, 3)
        copy_out(1)
        store_y(1, 2, y_sb[1])
        round_y_psum(0)
        mm_a(0, 2, False, False)
        mm_a(0, 3, True, False)
        mm_a(1, 2, False, True)
        mm_q(3, False, False)
        quant_xa(1, 3)
        round_y_psum(1)
        gate(2)
        mm_a(1, 3, False, True)
        turn(2, prod[2], False, True)
        gate(3, 0, 2)
        gate(3, 2, 4)
        quant_y(0)
        quant_y(1)
        store_words(0, 2)
        copy_out(2)
        store_y(2, 3, y_sb[2])
        turn(3, prod[3], False, True)
        copy_half(0)
        copy_half(1)
        store_y(3, 4, y_sb[3])
        round_y_psum(2)
        round_y(v_copy, 3)
        quant_y(2)
        quant_y(3)
        store_words(2, 4)
        for r in range(4):
            queue = nc.sync if r == 3 else nc.scalar
            queue.dma_start(out=out_2[0, r:16:4, :].bitcast(I32), in_=y_scale[r:P:32, :].bitcast(I32))
